import numpy as np, ml_dtypes
CORES = [1,3,5,9,11,13]
N = 6
GR, GC, HH, WW = 2, 3, 8, 32
def setup_inputs(rng):
    return {"x": rng.standard_normal((N, 128, HH * WW), dtype=np.float32).astype(ml_dtypes.bfloat16), "w": rng.standard_normal((N, 128, 9 * 128), dtype=np.float32).astype(ml_dtypes.bfloat16)}
def setup_inputs_big(rng):
    d = setup_inputs(rng)
    for k in ("x", "w"): d[k] = (d[k].astype(np.float32) * 1024.0).astype(d[k].dtype)
    return d
def setup_inputs_small(rng):
    d = setup_inputs(rng)
    for k in ("x", "w"): d[k] = (d[k].astype(np.float32) * (1 / 1024.0)).astype(d[k].dtype)
    return d
def setup_inputs_apart(rng):
    d = setup_inputs(rng)
    f = (10.0 ** rng.permutation(np.linspace(-1.5, 1.5, N))).astype(np.float32).reshape(N, 1, 1)
    for k in ("x", "w"): d[k] = (d[k].astype(np.float32) * f).astype(d[k].dtype)
    return d
def reference(x, w):
    X = x.astype(np.float64).reshape(GR, GC, 128, HH, WW); W = w.astype(np.float64)
    g = np.concatenate([np.concatenate(list(X[i]), axis=2) for i in range(GR)], axis=1)
    y = np.zeros((N, 128, HH * WW))
    for r in range(N):
        i0, j0 = HH * (r // GC), WW * (r % GC)
        for a in range(3):
            for b in range(3):
                sh = np.roll(g, (-2 * (a - 1), -2 * (b - 1)), axis=(1, 2))[:, i0:i0 + HH, j0:j0 + WW]
                y[r] += W[r][:, 128 * (3 * a + b):128 * (3 * a + b) + 128].T @ sh.reshape(128, HH * WW)
    return {"y": y.astype(ml_dtypes.bfloat16 if x.dtype != np.float64 else np.float64)}

@@ -1,0 +1,209 @@
+from concourse.bass import DstId, RemoteDMATransfer
+
+GC = 3
+BF, F32 = "bfloat16", "float32"
+SCRATCH = {
+    "S": ("sbuf", [128, 9, 16, 2], BF),
+    "HB": ("sbuf", [128, 32, 8, 2], BF),
+    "VH": ("sbuf", [128, 6, 16, 2], BF),
+    "LH": ("sbuf", [128, 8, 2], BF),
+    "RH": ("sbuf", [128, 8, 2], BF),
+    "W": ("sbuf", [128, 9, 128], BF),
+    "O": ("sbuf", [128, 8, 16, 2], BF),
+    "PT": ("psum", [128, 16, 16, 2], F32),
+    "PA": ("psum", [128, 16, 16, 2], F32),
+    "PB": ("psum", [128, 16, 16, 2], F32),
+}
+SEMAPHORES = ["ld", "ldm", "lw", "pk", "cp", "blk", "edge", "vh", "snt", "mT", "mA", "mB", "ov", "st"]
+
+ORDER = {"h": (0, 1, 2, 3, 4, 5, 6, 7), "a": (2, 3, 4, 5, 6, 7, 0, 1), "c": (6, 7, 0, 1, 2, 3, 4, 5)}
+BASE = {"h": 0, "a": 0, "c": 1}
+K_BLOCK = 8
+
+
+def _left(r):
+    return (r // GC) * GC + (r % GC - 1) % GC
+
+
+def _right(r):
+    return (r // GC) * GC + (r % GC + 1) % GC
+
+
+def _pick(mask, first, count):
+    bits = [b for b in range(32) if (mask >> b) & 1][first:first + count]
+    return sum(1 << b for b in bits)
+
+
+def _count(mask):
+    return sum((mask >> b) & 1 for b in range(32))
+
+
+def _segs(order, s0, n):
+    out = []
+    for k in range(n):
+        p = order.index(s0 + k)
+        if out and out[-1][1] + out[-1][2] == p:
+            out[-1][2] += 1
+        else:
+            out.append([k, p, 1])
+    return out
+
+
+def rank_program(g, core, T, topo):
+    rank = T.rank_of(core)
+    if rank is None:
+        return
+    cores, sem = T.cores, T.sem
+    n = len(cores)
+
+    def vert(r):
+        return (r + GC) % n
+
+    role = {}
+    for r in range(n):
+        row = [q for q in range(n) if q // GC == r // GC]
+        hub = [q for q in row if topo.may_write(cores[q], cores[vert(q)])][0]
+        role[r] = "h" if r == hub else ("a" if r == _left(hub) else "c")
+    me = role[rank]
+    hub = [q for q in range(n) if q // GC == rank // GC and role[q] == "h"][0]
+    ra, rc = _left(hub), _right(hub)
+    order, base = ORDER[me], BASE[me]
+
+    hub_off = topo.mask(cores[hub], cores[vert(hub)])
+    n_off = _count(hub_off)
+    half = n_off // 2
+
+    if me == "a":
+        g.sync.dma_start(T.S[:, 0:6], T.x[:, 64:256]).then_inc(sem.ld, 16)
+        g.scalar.dma_start(T.S[:, 6:8], T.x[:, 0:64]).then_inc(sem.ld, 16)
+        n_ld = 32
+    elif me == "c":
+        g.sync.dma_start(T.S[:, 3:9], T.x[:, 0:192]).then_inc(sem.ld, 16)
+        g.scalar.dma_start(T.S[:, 1:3], T.x[:, 192:256]).then_inc(sem.ld, 16)
+        n_ld = 32
+    else:
+        g.sync.dma_start(T.S[:, 0:8], T.x[:, :]).then_inc(sem.ld, 16)
+        g.scalar.dma_start(T.HB[:, 12:16], T.x[:, 192:256]).then_inc(sem.ldm, 16)
+        g.sync.dma_start(T.HB[:, 16:20], T.x[:, 0:64]).then_inc(sem.ldm, 16)
+        n_ld = 16
+    g.scalar.dma_start(T.W[:, :, :], T.w[:, :]).then_inc(sem.lw, 16)
+
+    if me == "a":
+        el, er = T.S[:, 8, 0:8, :], T.S[:, 8, 8:16, :]
+    elif me == "c":
+        el, er = T.S[:, 0, 0:8, :], T.S[:, 0, 8:16, :]
+    else:
+        el, er = T.HB[:, 0, :, :], T.HB[:, 31, :, :]
+    g.vector.wait_ge(sem.ld, n_ld)
+    g.vector.tensor_copy(el, T.S[:, base:base + 8, 0, :]).then_inc(sem.pk, 1)
+    g.vector.tensor_copy(er, T.S[:, base:base + 8, 15, :]).then_inc(sem.pk, 1)
+
+    def send(out_ap, in_ap, dst, mask, rsem):
+        rid, pid, _ = topo.addr(dst)
+        g.remote_dma(out_ap, in_ap, rsem, sem.snt, pid, rid, mask)
+        return _count(mask)
+
+    def transfer(out_ap, in_ap, dst, mask, rsem):
+        rid, pid, _ = topo.addr(dst)
+        return RemoteDMATransfer(dst_ids=[DstId(rid=rid, pnc=pid)], dma_engine_mask=mask, remote_sem=rsem,
+                                 src=in_ap, dst=out_ap)
+
+    n_blk = 2 * K_BLOCK
+    sent = 0
+    g.wait_ge(sem.pk, 2)
+    if me == "a":
+        sent += send(T.HB[:, 2:12], T.S[:, 4:9], cores[hub], _pick(topo.mask(core, cores[hub]), 0, K_BLOCK), sem.blk)
+        sent += send(T.RH[:, :, :], el, cores[rc], _pick(topo.mask(core, cores[rc]), 0, K_BLOCK), sem.edge)
+    elif me == "c":
+        sent += send(T.HB[:, 20:30], T.S[:, 0:5], cores[hub], _pick(topo.mask(core, cores[hub]), 0, K_BLOCK), sem.blk)
+        sent += send(T.LH[:, :, :], er, cores[ra], _pick(topo.mask(core, cores[ra]), 0, K_BLOCK), sem.edge)
+    else:
+        lo = _pick(hub_off & topo.mask(core, cores[ra]), 0, half)
+        hi = _pick(hub_off & topo.mask(core, cores[rc]), half, half)
+        g.remote_dma_fused([transfer(T.RH[:, :, :], el, cores[ra], lo, sem.edge),
+                            transfer(T.LH[:, :, :], er, cores[rc], hi, sem.edge)], local_sem=sem.snt)
+        sent += 2 * half
+        g.vector.wait_ge(sem.blk, n_blk)
+        g.vector.tensor_copy(T.HB[:, 1, :, :], T.HB[:, 21, :, :]).then_inc(sem.cp, 1)
+        g.vector.tensor_copy(T.HB[:, 30, :, :], T.HB[:, 10, :, :]).then_inc(sem.cp, 1)
+        g.wait_ge(sem.blk, n_blk)
+        g.wait_ge(sem.ldm, 32)
+        sent += send(T.VH[:, 0:6], T.HB[:, 10:22], cores[vert(hub)], hub_off, sem.vh)
+        g.wait_ge(sem.cp, 2)
+        g.remote_dma_fused([transfer(T.VH[:, 0:5], T.HB[:, 0:10], cores[vert(ra)], _pick(hub_off, 0, half), sem.vh),
+                            transfer(T.VH[:, 1:6], T.HB[:, 22:32], cores[vert(rc)], _pick(hub_off, half, half), sem.vh)],
+                           local_sem=sem.snt)
+        sent += 2 * half
+    g.wait_ge(sem.snt, sent)
+
+    if me == "h":
+        lget, lord = (lambda p, c: T.HB[:, 11, p:p + c, :]), ORDER["a"]
+        rget, rord = (lambda p, c: T.HB[:, 20, p:p + c, :]), ORDER["c"]
+        edge_sem, n_edge = sem.blk, n_blk
+    else:
+        lget, lord = (lambda p, c: T.LH[:, p:p + c, :]), ORDER[role[_left(rank)]]
+        rget, rord = (lambda p, c: T.RH[:, p:p + c, :]), ORDER[role[_right(rank)]]
+        edge_sem, n_edge = sem.edge, half + K_BLOCK
+    vrole = role[vert(rank)]
+    if vrole == "a":
+        cr, cl, n_vh = (0, 0, ORDER["h"]), (0, 8, ORDER["c"]), half
+    elif vrole == "h":
+        cl, cr, n_vh = (0, 8, ORDER["a"]), (5, 0, ORDER["c"]), n_off
+    else:
+        cr, cl, n_vh = (5, 0, ORDER["a"]), (5, 8, ORDER["h"]), half
+
+    banks = {"T": (T.PT, sem.mT, 0, 2), "A": (T.PA, sem.mA, 2, 4), "B": (T.PB, sem.mB, 6, 2)}
+    first, own, held, edges, verts = [], [], [], [], []
+    for G in ("A", "T", "B"):
+        P, _, g0, nr = banks[G]
+        for a in range(3):
+            s0 = g0 + 2 * (a - 1)
+            if 0 <= s0 <= 8 - nr:
+                runs = _segs(order, s0, nr)
+                for o, p, c in runs:
+                    q = base + p
+                    mid = (G, P[:, o:o + c, 0:16, :], 3 * a + 1, T.S[:, q:q + c, 0:16, :])
+                    if a == 1:
+                        first.append(mid)
+                    elif G == "A" and len(runs) == 1 and not held:
+                        held.append(mid)
+                    else:
+                        own.append(mid)
+                    own.append((G, P[:, o:o + c, 1:16, :], 3 * a, T.S[:, q:q + c, 0:15, :]))
+                    own.append((G, P[:, o:o + c, 0:15, :], 3 * a + 2, T.S[:, q:q + c, 1:16, :]))
+                for o, p, c in _segs(lord, s0, nr):
+                    edges.append((G, P[:, o:o + c, 0, :], 3 * a, lget(p, c)))
+                for o, p, c in _segs(rord, s0, nr):
+                    edges.append((G, P[:, o:o + c, 15, :], 3 * a + 2, rget(p, c)))
+            else:
+                v, srow = (1, 6) if s0 < 0 else (3, 0)
+                pl, pr = cl[1] + cl[2].index(srow), cr[1] + cr[2].index(srow)
+                verts.append((G, P[:, 0:2, 0, :], 3 * a, T.VH[:, cl[0], pl:pl + 2, :]))
+                verts.append((G, P[:, 0:2, 15, :], 3 * a + 2, T.VH[:, cr[0], pr:pr + 2, :]))
+                verts.append((G, P[:, 0:2, 1:16, :], 3 * a, T.VH[:, v:v + 2, 0:15, :]))
+                verts.append((G, P[:, 0:2, 0:15, :], 3 * a + 2, T.VH[:, v:v + 2, 1:16, :]))
+                verts.append((G, P[:, 0:2, 0:16, :], 3 * a + 1, T.VH[:, v:v + 2, 0:16, :]))
+    edges.sort(key=lambda m: 0 if m[0] == "A" else 1)
+    k_a = len([m for m in edges if m[0] == "A"])
+    edges = edges[:k_a] + held + edges[k_a:]
+    todo = first + own + edges + verts
+    last = {}
+    for i, m in enumerate(todo):
+        last[m[0]] = i
+    total = {G: len([m for m in todo if m[0] == G]) for G in banks}
+    g.tensor.wait_ge(sem.lw, 16)
+    g.tensor.wait_ge(sem.ld, n_ld)
+    for i, (G, out, tap, rhs) in enumerate(todo):
+        if i == len(first) + len(own):
+            g.tensor.wait_ge(edge_sem, n_edge)
+        if i == len(todo) - len(verts):
+            g.tensor.wait_ge(sem.vh, n_vh)
+        g.tensor.matmul(out, T.W[:, tap, :], rhs, i < len(first), i == last[G]).then_inc(banks[G][1], 1)
+
+    for G in ("A", "T", "B"):
+        P, s, g0, nr = banks[G]
+        g.vector.wait_ge(s, total[G])
+        g.vector.tensor_copy(T.O[:, g0:g0 + nr, :, :], P[:, 0:nr, :, :]).then_inc(sem.ov, 1)
+    g.sync.wait_ge(sem.ov, 3)
+    g.sync.dma_start(T.y[:, :], T.O[:, :, :, :]).then_inc(sem.st, 16)
+    g.sync.wait_ge(sem.st, 16)

@@ -4,8 +4,9 @@ GC = 3
 BF, F32 = "bfloat16", "float32"
 SCRATCH = {
     "S": ("sbuf", [128, 9, 16, 2], BF),
-    "HB": ("sbuf", [128, 32, 8, 2], BF),
-    "VH": ("sbuf", [128, 6, 16, 2], BF),
+    "HL": ("sbuf", [128, 7, 8, 2], BF),
+    "VH": ("sbuf", [128, 4, 16, 2], BF),
+    "CS": ("sbuf", [128, 2, 8, 2], BF),
     "LH": ("sbuf", [128, 8, 2], BF),
     "RH": ("sbuf", [128, 8, 2], BF),
     "W": ("sbuf", [128, 9, 128], BF),
@@ -14,11 +15,9 @@ SCRATCH = {
     "PA": ("psum", [128, 16, 16, 2], F32),
     "PB": ("psum", [128, 16, 16, 2], F32),
 }
-SEMAPHORES = ["ld", "ldm", "lw", "pk", "cp", "blk", "edge", "vh", "snt", "mT", "mA", "mB", "ov", "st"]
+SEMAPHORES = ["ld", "lw", "pk", "blk", "edge", "vh", "cs", "snt", "mT", "mA", "mB", "ov", "st"]
 
-ORDER = {"h": (0, 1, 2, 3, 4, 5, 6, 7), "a": (2, 3, 4, 5, 6, 7, 0, 1), "c": (6, 7, 0, 1, 2, 3, 4, 5)}
-BASE = {"h": 0, "a": 0, "c": 1}
-K_BLOCK = 8
+ORDER = (2, 3, 4, 5, 6, 7, 0, 1)
 
 
 def _left(r):
@@ -38,10 +37,10 @@ def _count(mask):
     return sum((mask >> b) & 1 for b in range(32))
 
 
-def _segs(order, s0, n):
+def _segs(s0, n):
     out = []
     for k in range(n):
-        p = order.index(s0 + k)
+        p = ORDER.index(s0 + k)
         if out and out[-1][1] + out[-1][2] == p:
             out[-1][2] += 1
         else:
@@ -50,53 +49,24 @@ def _segs(order, s0, n):
 
 
 def rank_program(g, core, T, topo):
-    rank = T.rank_of(core)
-    if rank is None:
-        return
     cores, sem = T.cores, T.sem
     n = len(cores)
 
     def vert(r):
         return (r + GC) % n
 
-    role = {}
+    role, via = {}, {}
     for r in range(n):
         row = [q for q in range(n) if q // GC == r // GC]
-        hub = [q for q in row if topo.may_write(cores[q], cores[vert(q)])][0]
-        role[r] = "h" if r == hub else ("a" if r == _left(hub) else "c")
-    me = role[rank]
-    hub = [q for q in range(n) if q // GC == rank // GC and role[q] == "h"][0]
-    ra, rc = _left(hub), _right(hub)
-    order, base = ORDER[me], BASE[me]
-
-    hub_off = topo.mask(cores[hub], cores[vert(hub)])
-    n_off = _count(hub_off)
-    half = n_off // 2
-
-    if me == "a":
-        g.sync.dma_start(T.S[:, 0:6], T.x[:, 64:256]).then_inc(sem.ld, 16)
-        g.scalar.dma_start(T.S[:, 6:8], T.x[:, 0:64]).then_inc(sem.ld, 16)
-        n_ld = 32
-    elif me == "c":
-        g.sync.dma_start(T.S[:, 3:9], T.x[:, 0:192]).then_inc(sem.ld, 16)
-        g.scalar.dma_start(T.S[:, 1:3], T.x[:, 192:256]).then_inc(sem.ld, 16)
-        n_ld = 32
-    else:
-        g.sync.dma_start(T.S[:, 0:8], T.x[:, :]).then_inc(sem.ld, 16)
-        g.scalar.dma_start(T.HB[:, 12:16], T.x[:, 192:256]).then_inc(sem.ldm, 16)
-        g.sync.dma_start(T.HB[:, 16:20], T.x[:, 0:64]).then_inc(sem.ldm, 16)
-        n_ld = 16
-    g.scalar.dma_start(T.W[:, :, :], T.w[:, :]).then_inc(sem.lw, 16)
-
-    if me == "a":
-        el, er = T.S[:, 8, 0:8, :], T.S[:, 8, 8:16, :]
-    elif me == "c":
-        el, er = T.S[:, 0, 0:8, :], T.S[:, 0, 8:16, :]
-    else:
-        el, er = T.HB[:, 0, :, :], T.HB[:, 31, :, :]
-    g.vector.wait_ge(sem.ld, n_ld)
-    g.vector.tensor_copy(el, T.S[:, base:base + 8, 0, :]).then_inc(sem.pk, 1)
-    g.vector.tensor_copy(er, T.S[:, base:base + 8, 15, :]).then_inc(sem.pk, 1)
+        h = [q for q in row if topo.may_write(cores[q], cores[vert(q)])][0]
+        role[r] = "h" if r == h else ("a" if r == _left(h) else "c")
+    for r in range(n):
+        if role[r] != "h":
+            idle = [k for k in range(topo.CORES_PER_CHIP * topo.CHIPS)
+                    if topo.chip(k) == topo.chip(cores[r]) and T.rank_of(k) is None
+                    and topo.may_write(k, cores[vert(r)]) and k not in via.values()]
+            idle.sort(key=lambda k: 0 if topo.die(k) == topo.die(cores[r]) else 1)
+            via[r] = idle[0]
 
     def send(out_ap, in_ap, dst, mask, rsem):
         rid, pid, _ = topo.addr(dst)
@@ -108,49 +78,80 @@ def rank_program(g, core, T, topo):
         return RemoteDMATransfer(dst_ids=[DstId(rid=rid, pnc=pid)], dma_engine_mask=mask, remote_sem=rsem,
                                  src=in_ap, dst=out_ap)
 
-    n_blk = 2 * K_BLOCK
-    sent = 0
-    g.wait_ge(sem.pk, 2)
-    if me == "a":
-        sent += send(T.HB[:, 2:12], T.S[:, 4:9], cores[hub], _pick(topo.mask(core, cores[hub]), 0, K_BLOCK), sem.blk)
-        sent += send(T.RH[:, :, :], el, cores[rc], _pick(topo.mask(core, cores[rc]), 0, K_BLOCK), sem.edge)
-    elif me == "c":
-        sent += send(T.HB[:, 20:30], T.S[:, 0:5], cores[hub], _pick(topo.mask(core, cores[hub]), 0, K_BLOCK), sem.blk)
-        sent += send(T.LH[:, :, :], er, cores[ra], _pick(topo.mask(core, cores[ra]), 0, K_BLOCK), sem.edge)
+    def split(src, dst_on, dst_off):
+        on, off = topo.mask(src, dst_on), topo.mask(src, dst_off)
+        return on & off, on & ~off
+
+    rank = T.rank_of(core)
+    if rank is None:
+        for r in via:
+            if via[r] == core:
+                lo, _ = split(cores[r], core, cores[vert(r)])
+                g.wait_ge(sem.blk, _count(lo))
+                k = send(T.VH[:, :, :, :], T.VH[:, :, :, :], cores[vert(r)], topo.mask(core, cores[vert(r)]), sem.vh)
+                g.wait_ge(sem.snt, k)
+        return
+
+    me = role[rank]
+    hub = [q for q in range(n) if q // GC == rank // GC and role[q] == "h"][0]
+    ra, rc = _left(hub), _right(hub)
+    other = rc if me == "a" else ra
+    far = cores[vert(rank)]
+
+    g.sync.dma_start(T.S[:, 0:6], T.x[:, 64:256]).then_inc(sem.ld, 16)
+    g.scalar.dma_start(T.S[:, 6:8], T.x[:, 0:64]).then_inc(sem.ld, 16)
+    g.scalar.dma_start(T.W[:, :, :], T.w[:, :]).then_inc(sem.lw, 16)
+
+    g.vector.wait_ge(sem.ld, 32)
+    if me == "h":
+        el, er, n_pk = T.HL[:, 0, :, :], T.HL[:, 1, :, :], 3
+        g.vector.tensor_copy(T.HL[:, 6, :, :], T.S[:, 0:8, 0, :]).then_inc(sem.pk, 1)
     else:
-        lo = _pick(hub_off & topo.mask(core, cores[ra]), 0, half)
-        hi = _pick(hub_off & topo.mask(core, cores[rc]), half, half)
-        g.remote_dma_fused([transfer(T.RH[:, :, :], el, cores[ra], lo, sem.edge),
-                            transfer(T.LH[:, :, :], er, cores[rc], hi, sem.edge)], local_sem=sem.snt)
-        sent += 2 * half
-        g.vector.wait_ge(sem.blk, n_blk)
-        g.vector.tensor_copy(T.HB[:, 1, :, :], T.HB[:, 21, :, :]).then_inc(sem.cp, 1)
-        g.vector.tensor_copy(T.HB[:, 30, :, :], T.HB[:, 10, :, :]).then_inc(sem.cp, 1)
+        el, er, n_pk = T.S[:, 8, 0:8, :], T.S[:, 8, 8:16, :], 2
+    g.vector.tensor_copy(el, T.S[:, 0:8, 0, :]).then_inc(sem.pk, 1)
+    g.vector.tensor_copy(er, T.S[:, 0:8, 15, :]).then_inc(sem.pk, 1)
+
+    lo_a, hi_a = split(cores[ra], cores[hub], cores[vert(ra)])
+    lo_c, hi_c = split(cores[rc], cores[hub], cores[vert(rc)])
+    n_blk = _count(hi_a) + _count(hi_c)
+    off_h, up_h = split(cores[hub], cores[ra], cores[vert(hub)])
+    n_off, half, uh = _count(off_h), _count(off_h) // 2, _count(up_h) // 2
+    sent = 0
+    g.wait_ge(sem.ld, 32)
+    if me != "h":
+        lo, hi = (lo_a, hi_a) if me == "a" else (lo_c, hi_c)
+        sent += send(T.VH[:, :, :, :], T.S[:, 4:8], via[rank], lo, sem.blk)
+        g.wait_ge(sem.pk, n_pk)
+        if me == "a":
+            sent += send(T.HL[:, 2:4], T.S[:, 8], cores[hub], hi, sem.blk)
+            sent += send(T.RH[:, :, :], el, cores[other], hi, sem.edge)
+        else:
+            sent += send(T.HL[:, 4:6], T.S[:, 8], cores[hub], hi, sem.blk)
+            sent += send(T.LH[:, :, :], er, cores[other], hi, sem.edge)
+    else:
+        sent += send(T.VH[:, :, :, :], T.S[:, 4:8], far, off_h, sem.vh)
+        g.wait_ge(sem.pk, n_pk)
+        g.remote_dma_fused([transfer(T.RH[:, :, :], el, cores[ra], _pick(up_h, 0, uh), sem.edge),
+                            transfer(T.LH[:, :, :], er, cores[rc], _pick(up_h, uh, uh), sem.edge)], local_sem=sem.snt)
+        sent += 2 * uh
         g.wait_ge(sem.blk, n_blk)
-        g.wait_ge(sem.ldm, 32)
-        sent += send(T.VH[:, 0:6], T.HB[:, 10:22], cores[vert(hub)], hub_off, sem.vh)
-        g.wait_ge(sem.cp, 2)
-        g.remote_dma_fused([transfer(T.VH[:, 0:5], T.HB[:, 0:10], cores[vert(ra)], _pick(hub_off, 0, half), sem.vh),
-                            transfer(T.VH[:, 1:6], T.HB[:, 22:32], cores[vert(rc)], _pick(hub_off, half, half), sem.vh)],
+        g.remote_dma_fused([transfer(T.CS[:, :, :, :], T.HL[:, 5:7], cores[vert(ra)], _pick(off_h, 0, half), sem.cs),
+                            transfer(T.CS[:, :, :, :], T.HL[:, 1:3], cores[vert(rc)], _pick(off_h, half, half), sem.cs)],
                            local_sem=sem.snt)
         sent += 2 * half
+        sent += send(T.CS[:, :, :, :], T.HL[:, 3:5], far, off_h, sem.cs)
     g.wait_ge(sem.snt, sent)
 
     if me == "h":
-        lget, lord = (lambda p, c: T.HB[:, 11, p:p + c, :]), ORDER["a"]
-        rget, rord = (lambda p, c: T.HB[:, 20, p:p + c, :]), ORDER["c"]
+        lget = lambda p, c: T.HL[:, 3, p:p + c, :]
+        rget = lambda p, c: T.HL[:, 4, p:p + c, :]
         edge_sem, n_edge = sem.blk, n_blk
     else:
-        lget, lord = (lambda p, c: T.LH[:, p:p + c, :]), ORDER[role[_left(rank)]]
-        rget, rord = (lambda p, c: T.RH[:, p:p + c, :]), ORDER[role[_right(rank)]]
-        edge_sem, n_edge = sem.edge, half + K_BLOCK
-    vrole = role[vert(rank)]
-    if vrole == "a":
-        cr, cl, n_vh = (0, 0, ORDER["h"]), (0, 8, ORDER["c"]), half
-    elif vrole == "h":
-        cl, cr, n_vh = (0, 8, ORDER["a"]), (5, 0, ORDER["c"]), n_off
-    else:
-        cr, cl, n_vh = (5, 0, ORDER["a"]), (5, 8, ORDER["h"]), half
+        lget = lambda p, c: T.LH[:, p:p + c, :]
+        rget = lambda p, c: T.RH[:, p:p + c, :]
+        edge_sem, n_edge = sem.edge, uh + _count(hi_c if me == "a" else hi_a)
+    n_vh = _count(topo.mask(cores[vert(rank)] if role[vert(rank)] == "h" else via[vert(rank)], core))
+    n_cs = n_off if role[vert(rank)] == "h" else half
 
     banks = {"T": (T.PT, sem.mT, 0, 2), "A": (T.PA, sem.mA, 2, 4), "B": (T.PB, sem.mB, 6, 2)}
     first, own, held, edges, verts = [], [], [], [], []
@@ -159,27 +160,23 @@ def rank_program(g, core, T, topo):
         for a in range(3):
             s0 = g0 + 2 * (a - 1)
             if 0 <= s0 <= 8 - nr:
-                runs = _segs(order, s0, nr)
+                runs = _segs(s0, nr)
                 for o, p, c in runs:
-                    q = base + p
-                    mid = (G, P[:, o:o + c, 0:16, :], 3 * a + 1, T.S[:, q:q + c, 0:16, :])
+                    mid = (G, P[:, o:o + c, 0:16, :], 3 * a + 1, T.S[:, p:p + c, 0:16, :])
                     if a == 1:
                         first.append(mid)
                     elif G == "A" and len(runs) == 1 and not held:
                         held.append(mid)
                     else:
                         own.append(mid)
-                    own.append((G, P[:, o:o + c, 1:16, :], 3 * a, T.S[:, q:q + c, 0:15, :]))
-                    own.append((G, P[:, o:o + c, 0:15, :], 3 * a + 2, T.S[:, q:q + c, 1:16, :]))
-                for o, p, c in _segs(lord, s0, nr):
+                    own.append((G, P[:, o:o + c, 1:16, :], 3 * a, T.S[:, p:p + c, 0:15, :]))
+                    own.append((G, P[:, o:o + c, 0:15, :], 3 * a + 2, T.S[:, p:p + c, 1:16, :]))
                     edges.append((G, P[:, o:o + c, 0, :], 3 * a, lget(p, c)))
-                for o, p, c in _segs(rord, s0, nr):
                     edges.append((G, P[:, o:o + c, 15, :], 3 * a + 2, rget(p, c)))
             else:
-                v, srow = (1, 6) if s0 < 0 else (3, 0)
-                pl, pr = cl[1] + cl[2].index(srow), cr[1] + cr[2].index(srow)
-                verts.append((G, P[:, 0:2, 0, :], 3 * a, T.VH[:, cl[0], pl:pl + 2, :]))
-                verts.append((G, P[:, 0:2, 15, :], 3 * a + 2, T.VH[:, cr[0], pr:pr + 2, :]))
+                v, q = (0, ORDER.index(6)) if s0 < 0 else (2, ORDER.index(0))
+                verts.append((G, P[:, 0:2, 0, :], 3 * a, T.CS[:, 0, q:q + 2, :]))
+                verts.append((G, P[:, 0:2, 15, :], 3 * a + 2, T.CS[:, 1, q:q + 2, :]))
                 verts.append((G, P[:, 0:2, 1:16, :], 3 * a, T.VH[:, v:v + 2, 0:15, :]))
                 verts.append((G, P[:, 0:2, 0:15, :], 3 * a + 2, T.VH[:, v:v + 2, 1:16, :]))
                 verts.append((G, P[:, 0:2, 0:16, :], 3 * a + 1, T.VH[:, v:v + 2, 0:16, :]))
@@ -192,12 +189,13 @@ def rank_program(g, core, T, topo):
         last[m[0]] = i
     total = {G: len([m for m in todo if m[0] == G]) for G in banks}
     g.tensor.wait_ge(sem.lw, 16)
-    g.tensor.wait_ge(sem.ld, n_ld)
+    g.tensor.wait_ge(sem.ld, 32)
     for i, (G, out, tap, rhs) in enumerate(todo):
         if i == len(first) + len(own):
             g.tensor.wait_ge(edge_sem, n_edge)
         if i == len(todo) - len(verts):
             g.tensor.wait_ge(sem.vh, n_vh)
+            g.tensor.wait_ge(sem.cs, n_cs)
         g.tensor.matmul(out, T.W[:, tap, :], rhs, i < len(first), i == last[G]).then_inc(banks[G][1], 1)
 
     for G in ("A", "T", "B"):

from concourse.bass import DstId, RemoteDMATransfer

GC = 3
BF, F32 = "bfloat16", "float32"
SCRATCH = {
    "S": ("sbuf", [128, 9, 16, 2], BF),
    "HL": ("sbuf", [128, 7, 8, 2], BF),
    "VH": ("sbuf", [128, 4, 16, 2], BF),
    "CS": ("sbuf", [128, 2, 8, 2], BF),
    "LH": ("sbuf", [128, 8, 2], BF),
    "RH": ("sbuf", [128, 8, 2], BF),
    "W": ("sbuf", [128, 9, 128], BF),
    "O": ("sbuf", [128, 8, 16, 2], BF),
    "PT": ("psum", [128, 16, 16, 2], F32),
    "PA": ("psum", [128, 16, 16, 2], F32),
    "PB": ("psum", [128, 16, 16, 2], F32),
}
SEMAPHORES = ["ld", "lw", "pk", "blk", "edge", "vh", "cs", "snt", "mT", "mA", "mB", "ov", "st"]

ORDER = (2, 3, 4, 5, 6, 7, 0, 1)


def _left(r):
    return (r // GC) * GC + (r % GC - 1) % GC


def _right(r):
    return (r // GC) * GC + (r % GC + 1) % GC


def _pick(mask, first, count):
    bits = [b for b in range(32) if (mask >> b) & 1][first:first + count]
    return sum(1 << b for b in bits)


def _count(mask):
    return sum((mask >> b) & 1 for b in range(32))


def _segs(s0, n):
    out = []
    for k in range(n):
        p = ORDER.index(s0 + k)
        if out and out[-1][1] + out[-1][2] == p:
            out[-1][2] += 1
        else:
            out.append([k, p, 1])
    return out


def rank_program(g, core, T, topo):
    cores, sem = T.cores, T.sem
    n = len(cores)

    def vert(r):
        return (r + GC) % n

    role, via = {}, {}
    for r in range(n):
        row = [q for q in range(n) if q // GC == r // GC]
        h = [q for q in row if topo.may_write(cores[q], cores[vert(q)])][0]
        role[r] = "h" if r == h else ("a" if r == _left(h) else "c")
    for r in range(n):
        if role[r] != "h":
            idle = [k for k in range(topo.CORES_PER_CHIP * topo.CHIPS)
                    if topo.chip(k) == topo.chip(cores[r]) and T.rank_of(k) is None
                    and topo.may_write(k, cores[vert(r)]) and k not in via.values()]
            idle.sort(key=lambda k: 0 if topo.die(k) == topo.die(cores[r]) else 1)
            via[r] = idle[0]

    def send(out_ap, in_ap, dst, mask, rsem):
        rid, pid, _ = topo.addr(dst)
        g.remote_dma(out_ap, in_ap, rsem, sem.snt, pid, rid, mask)
        return _count(mask)

    def transfer(out_ap, in_ap, dst, mask, rsem):
        rid, pid, _ = topo.addr(dst)
        return RemoteDMATransfer(dst_ids=[DstId(rid=rid, pnc=pid)], dma_engine_mask=mask, remote_sem=rsem,
                                 src=in_ap, dst=out_ap)

    def split(src, dst_on, dst_off):
        on, off = topo.mask(src, dst_on), topo.mask(src, dst_off)
        return on & off, on & ~off

    rank = T.rank_of(core)
    if rank is None:
        for r in via:
            if via[r] == core:
                lo, _ = split(cores[r], core, cores[vert(r)])
                g.wait_ge(sem.blk, _count(lo))
                k = send(T.VH[:, :, :, :], T.VH[:, :, :, :], cores[vert(r)], topo.mask(core, cores[vert(r)]), sem.vh)
                g.wait_ge(sem.snt, k)
        return

    me = role[rank]
    hub = [q for q in range(n) if q // GC == rank // GC and role[q] == "h"][0]
    ra, rc = _left(hub), _right(hub)
    other = rc if me == "a" else ra
    far = cores[vert(rank)]

    g.sync.dma_start(T.S[:, 0:6], T.x[:, 64:256]).then_inc(sem.ld, 16)
    g.scalar.dma_start(T.S[:, 6:8], T.x[:, 0:64]).then_inc(sem.ld, 16)
    g.scalar.dma_start(T.W[:, :, :], T.w[:, :]).then_inc(sem.lw, 16)

    g.vector.wait_ge(sem.ld, 32)
    if me == "h":
        el, er, n_pk = T.HL[:, 0, :, :], T.HL[:, 1, :, :], 3
        g.vector.tensor_copy(T.HL[:, 6, :, :], T.S[:, 0:8, 0, :]).then_inc(sem.pk, 1)
    else:
        el, er, n_pk = T.S[:, 8, 0:8, :], T.S[:, 8, 8:16, :], 2
    g.vector.tensor_copy(el, T.S[:, 0:8, 0, :]).then_inc(sem.pk, 1)
    g.vector.tensor_copy(er, T.S[:, 0:8, 15, :]).then_inc(sem.pk, 1)

    lo_a, hi_a = split(cores[ra], cores[hub], cores[vert(ra)])
    lo_c, hi_c = split(cores[rc], cores[hub], cores[vert(rc)])
    n_blk = _count(hi_a) + _count(hi_c)
    off_h, up_h = split(cores[hub], cores[ra], cores[vert(hub)])
    n_off, half, uh = _count(off_h), _count(off_h) // 2, _count(up_h) // 2
    sent = 0
    g.wait_ge(sem.ld, 32)
    if me != "h":
        lo, hi = (lo_a, hi_a) if me == "a" else (lo_c, hi_c)
        sent += send(T.VH[:, :, :, :], T.S[:, 4:8], via[rank], lo, sem.blk)
        g.wait_ge(sem.pk, n_pk)
        if me == "a":
            sent += send(T.HL[:, 2:4], T.S[:, 8], cores[hub], hi, sem.blk)
            sent += send(T.RH[:, :, :], el, cores[other], hi, sem.edge)
        else:
            sent += send(T.HL[:, 4:6], T.S[:, 8], cores[hub], hi, sem.blk)
            sent += send(T.LH[:, :, :], er, cores[other], hi, sem.edge)
    else:
        sent += send(T.VH[:, :, :, :], T.S[:, 4:8], far, off_h, sem.vh)
        g.wait_ge(sem.pk, n_pk)
        g.remote_dma_fused([transfer(T.RH[:, :, :], el, cores[ra], _pick(up_h, 0, uh), sem.edge),
                            transfer(T.LH[:, :, :], er, cores[rc], _pick(up_h, uh, uh), sem.edge)], local_sem=sem.snt)
        sent += 2 * uh
        g.wait_ge(sem.blk, n_blk)
        g.remote_dma_fused([transfer(T.CS[:, :, :, :], T.HL[:, 5:7], cores[vert(ra)], _pick(off_h, 0, half), sem.cs),
                            transfer(T.CS[:, :, :, :], T.HL[:, 1:3], cores[vert(rc)], _pick(off_h, half, half), sem.cs)],
                           local_sem=sem.snt)
        sent += 2 * half
        sent += send(T.CS[:, :, :, :], T.HL[:, 3:5], far, off_h, sem.cs)
    g.wait_ge(sem.snt, sent)

    if me == "h":
        lget = lambda p, c: T.HL[:, 3, p:p + c, :]
        rget = lambda p, c: T.HL[:, 4, p:p + c, :]
        edge_sem, n_edge = sem.blk, n_blk
    else:
        lget = lambda p, c: T.LH[:, p:p + c, :]
        rget = lambda p, c: T.RH[:, p:p + c, :]
        edge_sem, n_edge = sem.edge, uh + _count(hi_c if me == "a" else hi_a)
    n_vh = _count(topo.mask(cores[vert(rank)] if role[vert(rank)] == "h" else via[vert(rank)], core))
    n_cs = n_off if role[vert(rank)] == "h" else half

    banks = {"T": (T.PT, sem.mT, 0, 2), "A": (T.PA, sem.mA, 2, 4), "B": (T.PB, sem.mB, 6, 2)}
    first, own, held, edges, verts = [], [], [], [], []
    for G in ("A", "T", "B"):
        P, _, g0, nr = banks[G]
        for a in range(3):
            s0 = g0 + 2 * (a - 1)
            if 0 <= s0 <= 8 - nr:
                runs = _segs(s0, nr)
                for o, p, c in runs:
                    mid = (G, P[:, o:o + c, 0:16, :], 3 * a + 1, T.S[:, p:p + c, 0:16, :])
                    if a == 1:
                        first.append(mid)
                    elif G == "A" and len(runs) == 1 and not held:
                        held.append(mid)
                    else:
                        own.append(mid)
                    own.append((G, P[:, o:o + c, 1:16, :], 3 * a, T.S[:, p:p + c, 0:15, :]))
                    own.append((G, P[:, o:o + c, 0:15, :], 3 * a + 2, T.S[:, p:p + c, 1:16, :]))
                    edges.append((G, P[:, o:o + c, 0, :], 3 * a, lget(p, c)))
                    edges.append((G, P[:, o:o + c, 15, :], 3 * a + 2, rget(p, c)))
            else:
                v, q = (0, ORDER.index(6)) if s0 < 0 else (2, ORDER.index(0))
                verts.append((G, P[:, 0:2, 0, :], 3 * a, T.CS[:, 0, q:q + 2, :]))
                verts.append((G, P[:, 0:2, 15, :], 3 * a + 2, T.CS[:, 1, q:q + 2, :]))
                verts.append((G, P[:, 0:2, 1:16, :], 3 * a, T.VH[:, v:v + 2, 0:15, :]))
                verts.append((G, P[:, 0:2, 0:15, :], 3 * a + 2, T.VH[:, v:v + 2, 1:16, :]))
                verts.append((G, P[:, 0:2, 0:16, :], 3 * a + 1, T.VH[:, v:v + 2, 0:16, :]))
    edges.sort(key=lambda m: 0 if m[0] == "A" else 1)
    k_a = len([m for m in edges if m[0] == "A"])
    edges = edges[:k_a] + held + edges[k_a:]
    todo = first + own + edges + verts
    last = {}
    for i, m in enumerate(todo):
        last[m[0]] = i
    total = {G: len([m for m in todo if m[0] == G]) for G in banks}
    g.tensor.wait_ge(sem.lw, 16)
    g.tensor.wait_ge(sem.ld, 32)
    for i, (G, out, tap, rhs) in enumerate(todo):
        if i == len(first) + len(own):
            g.tensor.wait_ge(edge_sem, n_edge)
        if i == len(todo) - len(verts):
            g.tensor.wait_ge(sem.vh, n_vh)
            g.tensor.wait_ge(sem.cs, n_cs)
        g.tensor.matmul(out, T.W[:, tap, :], rhs, i < len(first), i == last[G]).then_inc(banks[G][1], 1)

    for G in ("A", "T", "B"):
        P, s, g0, nr = banks[G]
        g.vector.wait_ge(s, total[G])
        g.vector.tensor_copy(T.O[:, g0:g0 + nr, :, :], P[:, 0:nr, :, :]).then_inc(sem.ov, 1)
    g.sync.wait_ge(sem.ov, 3)
    g.sync.dma_start(T.y[:, :], T.O[:, :, :, :]).then_inc(sem.st, 16)
    g.sync.wait_ge(sem.st, 16)
